import numpy as np
import ml_dtypes


def mxq(x, axis, fmt="e4m3"):
    dtype, down = {"e4m3": (ml_dtypes.float8_e4m3fn, 7), "e5m2": (ml_dtypes.float8_e5m2, 14)}[fmt]
    v = np.moveaxis(np.asarray(x, np.float32).astype(ml_dtypes.bfloat16).astype(np.float64), axis, -1)
    blocks = v.reshape(v.shape[:-1] + (-1, 32))
    amax = np.abs(blocks).max(-1, keepdims=True)
    byte = np.maximum(np.where(amax > 0, np.frexp(amax)[1] - 1 + 127, 0) - down, 1)
    scale = np.exp2(byte - 127.0)
    codes = (blocks / scale).astype(np.float32).astype(dtype).astype(np.float64)
    return np.moveaxis((codes * scale).reshape(v.shape), -1, axis)


WIDE = False


def mx_kscale(k):
    if not WIDE:
        return np.ones(k)
    levels = np.array([10, -10, 5, -5, 0])
    if k % 512:
        return np.exp2(np.random.permutation(np.resize(levels, k // 32))).repeat(32)
    a = np.empty((k // 512, 16))
    for p in range(k // 512):
        a[p, :8] = np.random.permutation(np.resize(levels, 8))
        for g in range(8):
            far = levels[np.abs(levels - a[p, g]) >= 10]
            a[p, g + 8] = far[np.random.randint(len(far))]
    return np.exp2(a.ravel()).repeat(32)


def f64(x):
    return np.asarray(x).astype(np.float64)


def striped(idx):
    return np.tile(idx.reshape(-1, 16).T, (8, 1)).astype(np.uint16)


def unstriped(offs):
    return offs[:16].T.reshape(-1).astype(np.int64)


def pack_weight(w):
    k, n = w.shape
    w = f64(np.asarray(w, np.float32).astype(ml_dtypes.bfloat16)).reshape(k // 32, 32, n)
    amax = np.abs(w).max(1)
    byte = np.clip(np.where(amax > 0, np.frexp(amax)[1] - 1 + 127 - 7, 1), 1, 254)
    scaled = (w * np.exp2(127.0 - byte)[:, None, :]).reshape(k, n).astype(np.float32)
    words = np.ascontiguousarray(scaled.reshape(k // 512, 128, 4, n).transpose(0, 1, 3, 2)).astype(ml_dtypes.float8_e4m3fn).view(np.uint8)
    return words, np.ascontiguousarray(byte.astype(np.uint8).reshape(k // 512, 16, n))


def unpack_weight(words, scales):
    g, p, n, _ = words.shape
    vals = np.ascontiguousarray(words).view(ml_dtypes.float8_e4m3fn).astype(np.float64) * np.repeat(np.exp2(scales.astype(np.float64) - 127.0), 8, axis=1)[..., None]
    return vals.transpose(0, 1, 3, 2).reshape(g * 512, n)


K, T, S, D, H, V, Z, W = 512, 2048, 512, 2, 512, 256, 512, 2048
P = 2 ** 7


def setup_inputs():
    n = np.random.standard_normal
    s = mx_kscale(K)[:, None]
    packed_xT = pack_weight(n((K, T)) * s)
    packed_eT = pack_weight(n((K, W)) * s)
    return {
        "x_words": packed_xT[0],
        "x_scales": packed_xT[1],
        "w1": (n((K, H)) / np.sqrt(K) / s).astype(np.float32),
        "w2": (n((K, H)) / np.sqrt(K) / s).astype(np.float32),
        "e_words": packed_eT[0],
        "e_scales": packed_eT[1],
        "unit": (np.random.uniform(0.6, 1.4, (K, 1)) / np.sqrt(K) / s).astype(np.float32),
        "pop": (np.tile(np.random.uniform(0.3, 1.5, W), (P, 1))).astype(np.float32),
        "offs": striped(np.random.permutation(T)[:S]),
        "itm": striped(np.random.permutation(W)[:Z]),
        "sim": striped(np.random.permutation(V)),
    }


def reference(x_words, x_scales, w1, w2, e_words, e_scales, unit, pop, offs, itm, sim):
    xq = unpack_weight(x_words, x_scales)[:, unstriped(offs)]
    yd = mxq(f64(w2), 0, "e4m3").T @ xq
    att = np.exp(1.1 * np.tanh(yd))
    y = mxq(f64(w1), 0, "e4m3").T @ xq
    ay = att * y
    user = (ay.reshape(len(ay), -1, D).sum(axis=2)) / (att.reshape(len(att), -1, D).sum(axis=2))
    usr2 = user - (0.6 * user[:, unstriped(sim)])
    hid = f64(unit) * usr2
    e_itm = unpack_weight(e_words, e_scales)[:, unstriped(itm)]
    sc = mxq(hid, 0, "e4m3").T @ e_itm
    mu = sc.mean(axis=1, keepdims=True)
    return (sc - mu) / (f64(pop)[:1][:, unstriped(itm)])

@@ -1,0 +1,199 @@
+from contextlib import ExitStack
+
+import concourse.mybir as mybir
+from concourse.masks import make_identity
+
+F32 = mybir.dt.float32
+BF16 = mybir.dt.bfloat16
+I32 = mybir.dt.int32
+U32 = mybir.dt.uint32
+U16 = mybir.dt.uint16
+U8 = mybir.dt.uint8
+FP8X4 = mybir.dt.float8_e4m3fn_x4
+ALU = mybir.AluOpType
+ACT = mybir.ActivationFunctionType
+
+P = 128
+PACK = 4
+K = 512
+TABLE = 2048
+CLICKS = 512
+USERS = 256
+ITEMS = 512
+BLOCKS = USERS // P
+
+FLOPS = 2 * K * K * CLICKS * 2 + 2 * K * USERS * ITEMS
+BYTES = 2 * (K * TABLE + 16 * TABLE) + 2 * 4 * K * K + 4 * K + 4 * TABLE + 2 * P * 80 + 4 * USERS * ITEMS
+
+
+def tile_picked_yuserst_ips_p_kernel(
+    tc, x_words, x_scales, w1, w2, e_words, e_scales, unit, pop, offs, itm, sim, out
+):
+    nc = tc.nc
+    with ExitStack() as ctx:
+        keep = ctx.enter_context(tc.tile_pool(name="keep", bufs=1))
+        psum = ctx.enter_context(tc.psum_pool(name="psum", bufs=1))
+
+        def bank(b, shape):
+            return psum.tile(shape, F32, name="bank%d" % b, tag="bank%d" % b)
+
+        offs_sb = keep.tile([P, CLICKS // 16], U16, name="offs_sb")
+        itm_sb = keep.tile([P, ITEMS // 16], U16, name="itm_sb")
+        sim_sb = keep.tile([P, USERS // 16], U16, name="sim_sb")
+        x_word_table = keep.tile([P, TABLE], U32, name="x_word_table", align_bytes=64)
+        e_word_table = keep.tile([P, TABLE], U32, name="e_word_table", align_bytes=64)
+        x_scale_table = keep.tile([P, TABLE], U8, name="x_scale_table", align_bytes=64)
+        e_scale_table = keep.tile([P, TABLE], U8, name="e_scale_table", align_bytes=64)
+        w1_raw = keep.tile([P, PACK, K], F32, name="w1_raw", align_bytes=64)
+        w2_raw = keep.tile([P, PACK, K], F32, name="w2_raw", align_bytes=64)
+        unit_sb = keep.tile([P, PACK], F32, name="unit_sb")
+        pop_row = keep.tile([P, TABLE // P], F32, name="pop_row")
+
+        def load_words(table, words):
+            nc.sync.dma_start(out=table[:].bitcast(I32), in_=words[0].rearrange("p n r -> p (n r)").bitcast(I32))
+
+        def load_scales(table, scales):
+            nc.vector.memset(table[:].bitcast(I32), 0)
+            for q in range(4):
+                nc.scalar.dma_start(
+                    out=table[32 * q : 32 * q + 4, :].bitcast(I32), in_=scales[0, 4 * q : 4 * q + 4, :].bitcast(I32)
+                )
+
+        def load_weight(raw, w):
+            nc.sync.dma_start(out=raw[:], in_=w.rearrange("(p j) n -> p j n", j=PACK))
+
+        load_weight(w2_raw, w2)
+        nc.sync.dma_start(out=offs_sb[:], in_=offs)
+        nc.scalar.dma_start(out=pop_row[:], in_=pop[0].rearrange("(p c) -> p c", p=P))
+        load_scales(x_scale_table, x_scales)
+        load_words(x_word_table, x_words)
+        nc.sync.dma_start(out=itm_sb[:], in_=itm)
+        load_scales(e_scale_table, e_scales)
+        load_weight(w1_raw, w1)
+        nc.sync.dma_start(out=unit_sb[:], in_=unit.rearrange("(p t) o -> p (t o)", t=PACK))
+        nc.sync.dma_start(out=sim_sb[:], in_=sim)
+        load_words(e_word_table, e_words)
+
+        ident = keep.tile([P, P], F32, name="ident")
+        make_identity(nc, ident[:])
+        inv_row = keep.tile([P, TABLE // P], F32, name="inv_row")
+        nc.vector.reciprocal(out=inv_row[:], in_=pop_row[:])
+        inv_table = keep.tile([P, TABLE], F32, name="inv_table")
+        inv_table_lines = inv_table[:].rearrange("q (p b l) -> q b p l", b=4, l=4)
+        for b in range(4):
+            spread = bank(4 + b, [P, 4, P])
+            for l in range(4):
+                c = 4 * b + l
+                nc.tensor.transpose(spread[:, l, :], inv_row[:, c : c + 1].to_broadcast([P, P]), ident[:])
+            nc.scalar.copy(out=inv_table_lines[:, b], in_=spread[:].rearrange("q l p -> q p l"))
+
+        def gather_codes(name, table, dtype, offsets, count):
+            picked = keep.tile([P, count], dtype, name=name, align_bytes=64)
+            nc.vector.tensor_copy(out=picked[:], in_=table[:].indirect(offsets[:]))
+            return picked
+
+        def quantize_weight(name, raw):
+            dealt = keep.tile([P, PACK, P, PACK], BF16, name=name + "_dealt", align_bytes=64)
+            codes = keep.tile([P, K], U32, name=name + "_codes", align_bytes=64)
+            scales = keep.tile([P, K], U8, name=name + "_scales", align_bytes=64)
+            nc.vector.tensor_copy(
+                out=dealt[:].rearrange("p t m j -> p m j t"), in_=raw[:].rearrange("p j (m t) -> p m j t", t=PACK)
+            )
+            nc.vector.quantize_mx(
+                out=codes[:].bitcast(FP8X4), scales=scales[:], in_=dealt[:].rearrange("p t m j -> p (t m j)")
+            )
+            return codes, scales
+
+        x_scale = gather_codes("x_scale", x_scale_table, U8, offs_sb, CLICKS)
+        e_scale = gather_codes("e_scale", e_scale_table, U8, itm_sb, ITEMS)
+        w2_codes, w2_scales = quantize_weight("w2", w2_raw)
+        x_code = gather_codes("x_code", x_word_table, U32, offs_sb, CLICKS)
+
+        inv_pop = keep.tile([P, ITEMS], F32, name="inv_pop")
+        nc.scalar.activation(out=inv_pop[:], in_=inv_table[:].indirect(itm_sb[:]), func=ACT.Copy)
+
+        def layer(b, codes, scales, t):
+            acc = bank(b, [P, USERS, 2])
+            cols = slice(t * P, (t + 1) * P)
+            nc.tensor.matmul_mx(
+                out=acc[:].rearrange("p v d -> p (v d)"),
+                lhsT=codes[:, cols].bitcast(FP8X4),
+                lhsT_scale=scales[:, cols],
+                rhs=x_code[:].bitcast(FP8X4),
+                rhs_scale=x_scale[:],
+                start=True,
+                stop=True,
+            )
+            return acc
+
+        weight = []
+        for t in range(PACK):
+            yd = layer(t, w2_codes, w2_scales, t)
+            tanh_yd = keep.tile([P, 2, USERS], F32, name="tanh_yd%d" % t)
+            nc.scalar.activation(out=tanh_yd[:], in_=yd[:].rearrange("p v d -> p d v"), func=ACT.Tanh)
+            gap = keep.tile([P, USERS], F32, name="gap%d" % t)
+            nc.vector.tensor_tensor(out=gap[:], in0=tanh_yd[:, 0, :], in1=tanh_yd[:, 1, :], op=ALU.subtract)
+            share = keep.tile([P, USERS], F32, name="share%d" % t)
+            nc.scalar.activation(out=share[:], in_=gap[:], func=ACT.Sigmoid, scale=1.1)
+            weight.append(share)
+
+        w1_codes, w1_scales = quantize_weight("w1", w1_raw)
+
+        neg_user = keep.tile([P, PACK, USERS], F32, name="neg_user")
+        similar = [keep.tile([P, PACK, P], F32, name="similar%d" % h) for h in range(BLOCKS)]
+        for t in range(PACK):
+            y = layer(4 + t, w1_codes, w1_scales, t)
+            first = keep.tile([P, USERS], F32, name="first%d" % t)
+            second = keep.tile([P, USERS], F32, name="second%d" % t)
+            factor = unit_sb[:, t : t + 1]
+            nc.vector.scalar_tensor_tensor(
+                out=first[:], in0=y[:, :, 0], scalar=factor, in1=weight[t][:], op0=ALU.mult, op1=ALU.mult
+            )
+            nc.vector.scalar_tensor_tensor(
+                out=second[:], in0=weight[t][:], scalar=1.0, in1=y[:, :, 1], op0=ALU.subtract, op1=ALU.mult
+            )
+            nc.vector.scalar_tensor_tensor(
+                out=neg_user[:, t, :], in0=second[:], scalar=factor, in1=first[:], op0=ALU.mult, op1=ALU.subtract
+            )
+            for h in range(BLOCKS):
+                nc.scalar.activation(
+                    out=similar[h][:, t, :],
+                    in_=neg_user[:, t, :].indirect(sim_sb[:, 8 * h : 8 * (h + 1)]),
+                    func=ACT.Copy,
+                    scale=0.6,
+                )
+
+        e_code = gather_codes("e_code", e_word_table, U32, itm_sb, ITEMS)
+
+        for h in range(BLOCKS):
+            users = slice(h * P, (h + 1) * P)
+            hid = keep.tile([P, P, PACK], BF16, name="hid%d" % h, align_bytes=64)
+            nc.vector.tensor_tensor(
+                out=hid[:].rearrange("p (c i) t -> p c t i", i=4),
+                in0=similar[h][:].rearrange("p t (c i) -> p c t i", i=4),
+                in1=neg_user[:, :, users].rearrange("p t (c i) -> p c t i", i=4),
+                op=ALU.subtract,
+            )
+            hid_codes = keep.tile([P, P], U32, name="hid_codes%d" % h, align_bytes=64)
+            hid_scales = keep.tile([P, P], U8, name="hid_scales%d" % h, align_bytes=64)
+            nc.vector.quantize_mx(
+                out=hid_codes[:].bitcast(FP8X4), scales=hid_scales[:], in_=hid[:].rearrange("p v t -> p (v t)")
+            )
+            score = bank(h, [P, ITEMS])
+            nc.tensor.matmul_mx(
+                out=score[:],
+                lhsT=hid_codes[:].bitcast(FP8X4),
+                lhsT_scale=hid_scales[:],
+                rhs=e_code[:].bitcast(FP8X4),
+                rhs_scale=e_scale[:],
+                start=True,
+                stop=True,
+            )
+            scaled = keep.tile([P, ITEMS], BF16, name="scaled%d" % h)
+            mean = keep.tile([P, 1], F32, name="mean%d" % h)
+            nc.scalar.activation(out=scaled[:], in_=score[:], func=ACT.Copy, scale=1.0 / ITEMS, accum_out=mean[:])
+            result = keep.tile([P, ITEMS], F32, name="result%d" % h)
+            nc.vector.scalar_tensor_tensor(
+                out=result[:], in0=score[:], scalar=mean[:], in1=inv_pop[:], op0=ALU.subtract, op1=ALU.mult
+            )
+            nc.sync.dma_start(out=out[users, :], in_=result[:])

@@ -21,6 +21,7 @@ CLICKS = 512
 USERS = 256
 ITEMS = 512
 BLOCKS = USERS // P
+E_ROW0 = 4
 
 FLOPS = 2 * K * K * CLICKS * 2 + 2 * K * USERS * ITEMS
 BYTES = 2 * (K * TABLE + 16 * TABLE) + 2 * 4 * K * K + 4 * K + 4 * TABLE + 2 * P * 80 + 4 * USERS * ITEMS
@@ -44,32 +45,37 @@ def tile_picked_yuserst_ips_p_kernel(
         e_word_table = keep.tile([P, TABLE], U32, name="e_word_table", align_bytes=64)
         x_scale_table = keep.tile([P, TABLE], U8, name="x_scale_table", align_bytes=64)
         e_scale_table = keep.tile([P, TABLE], U8, name="e_scale_table", align_bytes=64)
-        w1_raw = keep.tile([P, PACK, K], F32, name="w1_raw", align_bytes=64)
-        w2_raw = keep.tile([P, PACK, K], F32, name="w2_raw", align_bytes=64)
+        w1_raw = [keep.tile([P, PACK, K // 2], F32, name="w1_raw%d" % u, align_bytes=64) for u in range(2)]
+        w2_raw = [keep.tile([P, PACK, K // 2], F32, name="w2_raw%d" % u, align_bytes=64) for u in range(2)]
         unit_sb = keep.tile([P, PACK], F32, name="unit_sb")
         pop_row = keep.tile([P, TABLE // P], F32, name="pop_row")
 
         def load_words(table, words):
             nc.sync.dma_start(out=table[:].bitcast(I32), in_=words[0].rearrange("p n r -> p (n r)").bitcast(I32))
 
-        def load_scales(table, scales):
-            nc.vector.memset(table[:].bitcast(I32), 0)
+        def load_scales(table, scales, row0):
             for q in range(4):
-                nc.scalar.dma_start(
-                    out=table[32 * q : 32 * q + 4, :].bitcast(I32), in_=scales[0, 4 * q : 4 * q + 4, :].bitcast(I32)
+                nc.sync.dma_start(
+                    out=table[32 * q + row0 : 32 * q + row0 + 4, :].bitcast(I32),
+                    in_=scales[0, 4 * q : 4 * q + 4, :].bitcast(I32),
                 )
 
-        def load_weight(raw, w):
-            nc.sync.dma_start(out=raw[:], in_=w.rearrange("(p j) n -> p j n", j=PACK))
+        def load_weight_half(raw, w, u):
+            rows = w.rearrange("(p j) n -> p j n", j=PACK)
+            nc.sync.dma_start(out=raw[u][:], in_=rows[:, :, u * (K // 2) : (u + 1) * (K // 2)])
 
-        load_weight(w2_raw, w2)
-        nc.sync.dma_start(out=offs_sb[:], in_=offs)
+        nc.vector.memset(x_scale_table[:].bitcast(I32), 0)
         nc.scalar.dma_start(out=pop_row[:], in_=pop[0].rearrange("(p c) -> p c", p=P))
-        load_scales(x_scale_table, x_scales)
-        load_words(x_word_table, x_words)
+        nc.gpsimd.memset(e_scale_table[:].bitcast(I32), 0)
+        nc.sync.dma_start(out=offs_sb[:], in_=offs)
+        load_weight_half(w2_raw, w2, 0)
+        load_scales(x_scale_table, x_scales, 0)
+        load_weight_half(w2_raw, w2, 1)
         nc.sync.dma_start(out=itm_sb[:], in_=itm)
-        load_scales(e_scale_table, e_scales)
-        load_weight(w1_raw, w1)
+        load_words(x_word_table, x_words)
+        load_scales(e_scale_table, e_scales, E_ROW0)
+        load_weight_half(w1_raw, w1, 0)
+        load_weight_half(w1_raw, w1, 1)
         nc.sync.dma_start(out=unit_sb[:], in_=unit.rearrange("(p t) o -> p (t o)", t=PACK))
         nc.sync.dma_start(out=sim_sb[:], in_=sim)
         load_words(e_word_table, e_words)
@@ -96,18 +102,24 @@ def tile_picked_yuserst_ips_p_kernel(
             dealt = keep.tile([P, PACK, P, PACK], BF16, name=name + "_dealt", align_bytes=64)
             codes = keep.tile([P, K], U32, name=name + "_codes", align_bytes=64)
             scales = keep.tile([P, K], U8, name=name + "_scales", align_bytes=64)
-            nc.vector.tensor_copy(
-                out=dealt[:].rearrange("p t m j -> p m j t"), in_=raw[:].rearrange("p j (m t) -> p m j t", t=PACK)
-            )
-            nc.vector.quantize_mx(
-                out=codes[:].bitcast(FP8X4), scales=scales[:], in_=dealt[:].rearrange("p t m j -> p (t m j)")
-            )
+            for u in range(2):
+                nc.vector.tensor_copy(
+                    out=dealt[:, :, u * (P // 2) : (u + 1) * (P // 2), :].rearrange("p t m j -> p m j t"),
+                    in_=raw[u][:].rearrange("p j (m t) -> p m j t", t=PACK),
+                )
+            for u in range(2):
+                cols = slice(u * 2 * P, (u + 1) * 2 * P)
+                nc.vector.quantize_mx(
+                    out=codes[:, cols].bitcast(FP8X4),
+                    scales=scales[:, cols],
+                    in_=dealt[:, 2 * u : 2 * u + 2].rearrange("p t m j -> p (t m j)"),
+                )
             return codes, scales
 
         x_scale = gather_codes("x_scale", x_scale_table, U8, offs_sb, CLICKS)
-        e_scale = gather_codes("e_scale", e_scale_table, U8, itm_sb, ITEMS)
         w2_codes, w2_scales = quantize_weight("w2", w2_raw)
         x_code = gather_codes("x_code", x_word_table, U32, offs_sb, CLICKS)
+        e_scale = gather_codes("e_scale", e_scale_table, U8, itm_sb, ITEMS)
 
         inv_pop = keep.tile([P, ITEMS], F32, name="inv_pop")
         nc.scalar.activation(out=inv_pop[:], in_=inv_table[:].indirect(itm_sb[:]), func=ACT.Copy)
@@ -130,11 +142,11 @@ def tile_picked_yuserst_ips_p_kernel(
         for t in range(PACK):
             yd = layer(t, w2_codes, w2_scales, t)
             tanh_yd = keep.tile([P, 2, USERS], F32, name="tanh_yd%d" % t)
-            nc.scalar.activation(out=tanh_yd[:], in_=yd[:].rearrange("p v d -> p d v"), func=ACT.Tanh)
+            nc.scalar.activation(out=tanh_yd[:], in_=yd[:].rearrange("p v d -> p d v"), func=ACT.Sigmoid, scale=2.0)
             gap = keep.tile([P, USERS], F32, name="gap%d" % t)
             nc.vector.tensor_tensor(out=gap[:], in0=tanh_yd[:, 0, :], in1=tanh_yd[:, 1, :], op=ALU.subtract)
             share = keep.tile([P, USERS], F32, name="share%d" % t)
-            nc.scalar.activation(out=share[:], in_=gap[:], func=ACT.Sigmoid, scale=1.1)
+            nc.scalar.activation(out=share[:], in_=gap[:], func=ACT.Sigmoid, scale=2.2)
             weight.append(share)
 
         w1_codes, w1_scales = quantize_weight("w1", w1_raw)
@@ -185,7 +197,7 @@ def tile_picked_yuserst_ips_p_kernel(
                 lhsT=hid_codes[:].bitcast(FP8X4),
                 lhsT_scale=hid_scales[:],
                 rhs=e_code[:].bitcast(FP8X4),
-                rhs_scale=e_scale[:],
+                rhs_scale=e_scale[E_ROW0:, :],
                 start=True,
                 stop=True,
             )
@@ -196,4 +208,4 @@ def tile_picked_yuserst_ips_p_kernel(
             nc.vector.scalar_tensor_tensor(
                 out=result[:], in0=score[:], scalar=mean[:], in1=inv_pop[:], op0=ALU.subtract, op1=ALU.mult
             )
-            nc.sync.dma_start(out=out[users, :], in_=result[:])
+            [nc.sync, nc.scalar][h].dma_start(out=out[users, :], in_=result[:])

@@ -41,50 +41,47 @@ def tile_picked_yuserst_ips_p_kernel(
         offs_sb = keep.tile([P, CLICKS // 16], U16, name="offs_sb")
         itm_sb = keep.tile([P, ITEMS // 16], U16, name="itm_sb")
         sim_sb = keep.tile([P, USERS // 16], U16, name="sim_sb")
-        x_word_table = keep.tile([P, TABLE], U32, name="x_word_table", align_bytes=64)
-        e_word_table = keep.tile([P, TABLE], U32, name="e_word_table", align_bytes=64)
         x_scale_table = keep.tile([P, TABLE], U8, name="x_scale_table", align_bytes=64)
         e_scale_table = keep.tile([P, TABLE], U8, name="e_scale_table", align_bytes=64)
-        w1_raw = [keep.tile([P, PACK, K // 2], F32, name="w1_raw%d" % u, align_bytes=64) for u in range(2)]
-        w2_raw = [keep.tile([P, PACK, K // 2], F32, name="w2_raw%d" % u, align_bytes=64) for u in range(2)]
         unit_sb = keep.tile([P, PACK], F32, name="unit_sb")
-        pop_row = keep.tile([P, TABLE // P], F32, name="pop_row")
 
-        def load_words(table, words):
+        def load_words(name, tag, words):
+            table = keep.tile([P, TABLE], U32, name=name, tag=tag, align_bytes=64)
             nc.sync.dma_start(out=table[:].bitcast(I32), in_=words[0].rearrange("p n r -> p (n r)").bitcast(I32))
+            return table
 
-        def load_scales(table, scales, row0):
+        def load_scales(table, scales, row0, queues):
             for q in range(4):
-                nc.sync.dma_start(
+                queues[q].dma_start(
                     out=table[32 * q + row0 : 32 * q + row0 + 4, :].bitcast(I32),
                     in_=scales[0, 4 * q : 4 * q + 4, :].bitcast(I32),
                 )
 
-        def load_weight_half(raw, w, u):
+        def load_weight_half(name, w, u):
             rows = w.rearrange("(p j) n -> p j n", j=PACK)
-            nc.sync.dma_start(out=raw[u][:], in_=rows[:, :, u * (K // 2) : (u + 1) * (K // 2)])
+            half = keep.tile([P, PACK, K // 2], F32, name="%s_raw%d" % (name, u), tag="raw%d" % u, align_bytes=64)
+            nc.sync.dma_start(out=half[:], in_=rows[:, :, u * (K // 2) : (u + 1) * (K // 2)])
+            return half
 
         nc.vector.memset(x_scale_table[:].bitcast(I32), 0)
-        nc.scalar.dma_start(out=pop_row[:], in_=pop[0].rearrange("(p c) -> p c", p=P))
         nc.gpsimd.memset(e_scale_table[:].bitcast(I32), 0)
+        pop_row = keep.tile([P, TABLE // P], F32, name="pop_row")
+        nc.scalar.dma_start(out=pop_row[:], in_=pop[0].rearrange("(p c) -> p c", p=P))
         nc.sync.dma_start(out=offs_sb[:], in_=offs)
-        load_weight_half(w2_raw, w2, 0)
-        load_scales(x_scale_table, x_scales, 0)
-        load_weight_half(w2_raw, w2, 1)
+        w2_raw = [load_weight_half("w2", w2, 0)]
+        load_scales(x_scale_table, x_scales, 0, [nc.sync] * 4)
+        w2_raw.append(load_weight_half("w2", w2, 1))
         nc.sync.dma_start(out=itm_sb[:], in_=itm)
-        load_words(x_word_table, x_words)
-        load_scales(e_scale_table, e_scales, E_ROW0)
-        load_weight_half(w1_raw, w1, 0)
-        load_weight_half(w1_raw, w1, 1)
-        nc.sync.dma_start(out=unit_sb[:], in_=unit.rearrange("(p t) o -> p (t o)", t=PACK))
-        nc.sync.dma_start(out=sim_sb[:], in_=sim)
-        load_words(e_word_table, e_words)
+        x_word_table = load_words("x_word_table", "x_words", x_words)
+        load_scales(e_scale_table, e_scales, E_ROW0, [nc.sync] * 4)
 
         ident = keep.tile([P, P], F32, name="ident")
         make_identity(nc, ident[:])
+        warm = keep.tile([P, 1], F32, name="warm")
+        nc.scalar.activation(out=warm[:], in_=ident[:, 0:1], func=ACT.Sigmoid)
         inv_row = keep.tile([P, TABLE // P], F32, name="inv_row")
         nc.vector.reciprocal(out=inv_row[:], in_=pop_row[:])
-        inv_table = keep.tile([P, TABLE], F32, name="inv_table")
+        inv_table = keep.tile([P, TABLE], F32, name="inv_table", tag="w1_dealt", align_bytes=64)
         inv_table_lines = inv_table[:].rearrange("q (p b l) -> q b p l", b=4, l=4)
         for b in range(4):
             spread = bank(4 + b, [P, 4, P])
@@ -93,17 +90,20 @@ def tile_picked_yuserst_ips_p_kernel(
                 nc.tensor.transpose(spread[:, l, :], inv_row[:, c : c + 1].to_broadcast([P, P]), ident[:])
             nc.scalar.copy(out=inv_table_lines[:, b], in_=spread[:].rearrange("q l p -> q p l"))
 
+        inv_pop = keep.tile([P, ITEMS], F32, name="inv_pop")
+        nc.scalar.activation(out=inv_pop[:], in_=inv_table[:].indirect(itm_sb[:]), func=ACT.Copy)
+
         def gather_codes(name, table, dtype, offsets, count):
             picked = keep.tile([P, count], dtype, name=name, align_bytes=64)
             nc.vector.tensor_copy(out=picked[:], in_=table[:].indirect(offsets[:]))
             return picked
 
-        def quantize_weight(name, raw):
-            dealt = keep.tile([P, PACK, P, PACK], BF16, name=name + "_dealt", align_bytes=64)
+        def quantize_weight(name, raw, copies):
+            dealt = keep.tile([P, PACK, P, PACK], BF16, name=name + "_dealt", tag=name + "_dealt", align_bytes=64)
             codes = keep.tile([P, K], U32, name=name + "_codes", align_bytes=64)
             scales = keep.tile([P, K], U8, name=name + "_scales", align_bytes=64)
             for u in range(2):
-                nc.vector.tensor_copy(
+                copies[u](
                     out=dealt[:, :, u * (P // 2) : (u + 1) * (P // 2), :].rearrange("p t m j -> p m j t"),
                     in_=raw[u][:].rearrange("p j (m t) -> p m j t", t=PACK),
                 )
@@ -117,12 +117,14 @@ def tile_picked_yuserst_ips_p_kernel(
             return codes, scales
 
         x_scale = gather_codes("x_scale", x_scale_table, U8, offs_sb, CLICKS)
-        w2_codes, w2_scales = quantize_weight("w2", w2_raw)
+        w2_codes, w2_scales = quantize_weight("w2", w2_raw, [nc.vector.tensor_copy, nc.vector.tensor_copy])
+        w1_raw = [load_weight_half("w1", w1, u) for u in range(2)]
+        nc.sync.dma_start(out=unit_sb[:], in_=unit.rearrange("(p t) o -> p (t o)", t=PACK))
+        nc.sync.dma_start(out=sim_sb[:], in_=sim)
+        e_word_table = load_words("e_word_table", "w2_dealt", e_words)
         x_code = gather_codes("x_code", x_word_table, U32, offs_sb, CLICKS)
+        w1_codes, w1_scales = quantize_weight("w1", w1_raw, [nc.scalar.copy, nc.vector.tensor_copy])
         e_scale = gather_codes("e_scale", e_scale_table, U8, itm_sb, ITEMS)
-
-        inv_pop = keep.tile([P, ITEMS], F32, name="inv_pop")
-        nc.scalar.activation(out=inv_pop[:], in_=inv_table[:].indirect(itm_sb[:]), func=ACT.Copy)
 
         def layer(b, codes, scales, t):
             acc = bank(b, [P, USERS, 2])
@@ -139,24 +141,22 @@ def tile_picked_yuserst_ips_p_kernel(
             return acc
 
         weight = []
+        squash = keep.tile([P, PACK, 2, USERS], F32, name="squash", tag="raw0", align_bytes=64)
+        gap = keep.tile([P, PACK, USERS], F32, name="gap", tag="w1_dealt", align_bytes=64)
         for t in range(PACK):
             yd = layer(t, w2_codes, w2_scales, t)
-            tanh_yd = keep.tile([P, 2, USERS], F32, name="tanh_yd%d" % t)
-            nc.scalar.activation(out=tanh_yd[:], in_=yd[:].rearrange("p v d -> p d v"), func=ACT.Sigmoid, scale=2.0)
-            gap = keep.tile([P, USERS], F32, name="gap%d" % t)
-            nc.vector.tensor_tensor(out=gap[:], in0=tanh_yd[:, 0, :], in1=tanh_yd[:, 1, :], op=ALU.subtract)
+            nc.scalar.activation(out=squash[:, t], in_=yd[:].rearrange("p v d -> p d v"), func=ACT.Sigmoid, scale=2.0)
+            nc.vector.tensor_tensor(out=gap[:, t, :], in0=squash[:, t, 0, :], in1=squash[:, t, 1, :], op=ALU.subtract)
             share = keep.tile([P, USERS], F32, name="share%d" % t)
-            nc.scalar.activation(out=share[:], in_=gap[:], func=ACT.Sigmoid, scale=2.2)
+            nc.scalar.activation(out=share[:], in_=gap[:, t, :], func=ACT.Sigmoid, scale=2.2)
             weight.append(share)
-
-        w1_codes, w1_scales = quantize_weight("w1", w1_raw)
 
         neg_user = keep.tile([P, PACK, USERS], F32, name="neg_user")
         similar = [keep.tile([P, PACK, P], F32, name="similar%d" % h) for h in range(BLOCKS)]
         for t in range(PACK):
             y = layer(4 + t, w1_codes, w1_scales, t)
             first = keep.tile([P, USERS], F32, name="first%d" % t)
-            second = keep.tile([P, USERS], F32, name="second%d" % t)
+            second = keep.tile([P, USERS], F32, name="second%d" % t, tag="second%d" % t, align_bytes=64)
             factor = unit_sb[:, t : t + 1]
             nc.vector.scalar_tensor_tensor(
                 out=first[:], in0=y[:, :, 0], scalar=factor, in1=weight[t][:], op0=ALU.mult, op1=ALU.mult
@@ -175,7 +175,11 @@ def tile_picked_yuserst_ips_p_kernel(
                     scale=0.6,
                 )
 
-        e_code = gather_codes("e_code", e_word_table, U32, itm_sb, ITEMS)
+        e_code = []
+        for u in range(2):
+            picked = keep.tile([P, ITEMS // 2], U32, name="e_code%d" % u, tag=["e_code0", "second3"][u], align_bytes=64)
+            nc.vector.tensor_copy(out=picked[:], in_=e_word_table[:].indirect(itm_sb[:, 16 * u : 16 * (u + 1)]))
+            e_code.append(picked)
 
         for h in range(BLOCKS):
             users = slice(h * P, (h + 1) * P)
@@ -192,20 +196,25 @@ def tile_picked_yuserst_ips_p_kernel(
                 out=hid_codes[:].bitcast(FP8X4), scales=hid_scales[:], in_=hid[:].rearrange("p v t -> p (v t)")
             )
             score = bank(h, [P, ITEMS])
-            nc.tensor.matmul_mx(
-                out=score[:],
-                lhsT=hid_codes[:].bitcast(FP8X4),
-                lhsT_scale=hid_scales[:],
-                rhs=e_code[:].bitcast(FP8X4),
-                rhs_scale=e_scale[E_ROW0:, :],
-                start=True,
-                stop=True,
-            )
+            for u in range(2):
+                items = slice(u * ITEMS // 2, (u + 1) * ITEMS // 2)
+                nc.tensor.matmul_mx(
+                    out=score[:, items],
+                    lhsT=hid_codes[:].bitcast(FP8X4),
+                    lhsT_scale=hid_scales[:],
+                    rhs=e_code[u][:].bitcast(FP8X4),
+                    rhs_scale=e_scale[E_ROW0:, items],
+                    start=True,
+                    stop=True,
+                )
             scaled = keep.tile([P, ITEMS], BF16, name="scaled%d" % h)
             mean = keep.tile([P, 1], F32, name="mean%d" % h)
             nc.scalar.activation(out=scaled[:], in_=score[:], func=ACT.Copy, scale=1.0 / ITEMS, accum_out=mean[:])
-            result = keep.tile([P, ITEMS], F32, name="result%d" % h)
-            nc.vector.scalar_tensor_tensor(
-                out=result[:], in0=score[:], scalar=mean[:], in1=inv_pop[:], op0=ALU.subtract, op1=ALU.mult
-            )
-            [nc.sync, nc.scalar][h].dma_start(out=out[users, :], in_=result[:])
+            for u in range(1 + h):
+                width = ITEMS // (1 + h)
+                items = slice(u * width, (u + 1) * width)
+                result = keep.tile([P, width], F32, name="result%d_%d" % (h, u))
+                nc.vector.scalar_tensor_tensor(
+                    out=result[:], in0=score[:, items], scalar=mean[:], in1=inv_pop[:, items], op0=ALU.subtract, op1=ALU.mult
+                )
+                [nc.sync, nc.scalar][(h + u) % 2].dma_start(out=out[users, items], in_=result[:])

from contextlib import ExitStack

import concourse.mybir as mybir
from concourse.masks import make_identity

F32 = mybir.dt.float32
BF16 = mybir.dt.bfloat16
I32 = mybir.dt.int32
U32 = mybir.dt.uint32
U16 = mybir.dt.uint16
U8 = mybir.dt.uint8
FP8X4 = mybir.dt.float8_e4m3fn_x4
ALU = mybir.AluOpType
ACT = mybir.ActivationFunctionType

P = 128
PACK = 4
K = 512
TABLE = 2048
CLICKS = 512
USERS = 256
ITEMS = 512
BLOCKS = USERS // P
E_ROW0 = 4

FLOPS = 2 * K * K * CLICKS * 2 + 2 * K * USERS * ITEMS
BYTES = 2 * (K * TABLE + 16 * TABLE) + 2 * 4 * K * K + 4 * K + 4 * TABLE + 2 * P * 80 + 4 * USERS * ITEMS


def tile_picked_yuserst_ips_p_kernel(
    tc, x_words, x_scales, w1, w2, e_words, e_scales, unit, pop, offs, itm, sim, out
):
    nc = tc.nc
    with ExitStack() as ctx:
        keep = ctx.enter_context(tc.tile_pool(name="keep", bufs=1))
        psum = ctx.enter_context(tc.psum_pool(name="psum", bufs=1))

        def bank(b, shape):
            return psum.tile(shape, F32, name="bank%d" % b, tag="bank%d" % b)

        offs_sb = keep.tile([P, CLICKS // 16], U16, name="offs_sb")
        itm_sb = keep.tile([P, ITEMS // 16], U16, name="itm_sb")
        sim_sb = keep.tile([P, USERS // 16], U16, name="sim_sb")
        x_scale_table = keep.tile([P, TABLE], U8, name="x_scale_table", align_bytes=64)
        e_scale_table = keep.tile([P, TABLE], U8, name="e_scale_table", align_bytes=64)
        unit_sb = keep.tile([P, PACK], F32, name="unit_sb")

        def load_words(name, tag, words):
            table = keep.tile([P, TABLE], U32, name=name, tag=tag, align_bytes=64)
            nc.sync.dma_start(out=table[:].bitcast(I32), in_=words[0].rearrange("p n r -> p (n r)").bitcast(I32))
            return table

        def load_scales(table, scales, row0, queues):
            for q in range(4):
                queues[q].dma_start(
                    out=table[32 * q + row0 : 32 * q + row0 + 4, :].bitcast(I32),
                    in_=scales[0, 4 * q : 4 * q + 4, :].bitcast(I32),
                )

        def load_weight_half(name, w, u):
            rows = w.rearrange("(p j) n -> p j n", j=PACK)
            half = keep.tile([P, PACK, K // 2], F32, name="%s_raw%d" % (name, u), tag="raw%d" % u, align_bytes=64)
            nc.sync.dma_start(out=half[:], in_=rows[:, :, u * (K // 2) : (u + 1) * (K // 2)])
            return half

        nc.vector.memset(x_scale_table[:].bitcast(I32), 0)
        nc.gpsimd.memset(e_scale_table[:].bitcast(I32), 0)
        pop_row = keep.tile([P, TABLE // P], F32, name="pop_row")
        nc.scalar.dma_start(out=pop_row[:], in_=pop[0].rearrange("(p c) -> p c", p=P))
        nc.sync.dma_start(out=offs_sb[:], in_=offs)
        w2_raw = [load_weight_half("w2", w2, 0)]
        load_scales(x_scale_table, x_scales, 0, [nc.sync] * 4)
        w2_raw.append(load_weight_half("w2", w2, 1))
        nc.sync.dma_start(out=itm_sb[:], in_=itm)
        x_word_table = load_words("x_word_table", "x_words", x_words)
        load_scales(e_scale_table, e_scales, E_ROW0, [nc.sync] * 4)

        ident = keep.tile([P, P], F32, name="ident")
        make_identity(nc, ident[:])
        warm = keep.tile([P, 1], F32, name="warm")
        nc.scalar.activation(out=warm[:], in_=ident[:, 0:1], func=ACT.Sigmoid)
        inv_row = keep.tile([P, TABLE // P], F32, name="inv_row")
        nc.vector.reciprocal(out=inv_row[:], in_=pop_row[:])
        inv_table = keep.tile([P, TABLE], F32, name="inv_table", tag="w1_dealt", align_bytes=64)
        inv_table_lines = inv_table[:].rearrange("q (p b l) -> q b p l", b=4, l=4)
        for b in range(4):
            spread = bank(4 + b, [P, 4, P])
            for l in range(4):
                c = 4 * b + l
                nc.tensor.transpose(spread[:, l, :], inv_row[:, c : c + 1].to_broadcast([P, P]), ident[:])
            nc.scalar.copy(out=inv_table_lines[:, b], in_=spread[:].rearrange("q l p -> q p l"))

        inv_pop = keep.tile([P, ITEMS], F32, name="inv_pop")
        nc.scalar.activation(out=inv_pop[:], in_=inv_table[:].indirect(itm_sb[:]), func=ACT.Copy)

        def gather_codes(name, table, dtype, offsets, count):
            picked = keep.tile([P, count], dtype, name=name, align_bytes=64)
            nc.vector.tensor_copy(out=picked[:], in_=table[:].indirect(offsets[:]))
            return picked

        def quantize_weight(name, raw, copies):
            dealt = keep.tile([P, PACK, P, PACK], BF16, name=name + "_dealt", tag=name + "_dealt", align_bytes=64)
            codes = keep.tile([P, K], U32, name=name + "_codes", align_bytes=64)
            scales = keep.tile([P, K], U8, name=name + "_scales", align_bytes=64)
            for u in range(2):
                copies[u](
                    out=dealt[:, :, u * (P // 2) : (u + 1) * (P // 2), :].rearrange("p t m j -> p m j t"),
                    in_=raw[u][:].rearrange("p j (m t) -> p m j t", t=PACK),
                )
            for u in range(2):
                cols = slice(u * 2 * P, (u + 1) * 2 * P)
                nc.vector.quantize_mx(
                    out=codes[:, cols].bitcast(FP8X4),
                    scales=scales[:, cols],
                    in_=dealt[:, 2 * u : 2 * u + 2].rearrange("p t m j -> p (t m j)"),
                )
            return codes, scales

        x_scale = gather_codes("x_scale", x_scale_table, U8, offs_sb, CLICKS)
        w2_codes, w2_scales = quantize_weight("w2", w2_raw, [nc.vector.tensor_copy, nc.vector.tensor_copy])
        w1_raw = [load_weight_half("w1", w1, u) for u in range(2)]
        nc.sync.dma_start(out=unit_sb[:], in_=unit.rearrange("(p t) o -> p (t o)", t=PACK))
        nc.sync.dma_start(out=sim_sb[:], in_=sim)
        e_word_table = load_words("e_word_table", "w2_dealt", e_words)
        x_code = gather_codes("x_code", x_word_table, U32, offs_sb, CLICKS)
        w1_codes, w1_scales = quantize_weight("w1", w1_raw, [nc.scalar.copy, nc.vector.tensor_copy])
        e_scale = gather_codes("e_scale", e_scale_table, U8, itm_sb, ITEMS)

        def layer(b, codes, scales, t):
            acc = bank(b, [P, USERS, 2])
            cols = slice(t * P, (t + 1) * P)
            nc.tensor.matmul_mx(
                out=acc[:].rearrange("p v d -> p (v d)"),
                lhsT=codes[:, cols].bitcast(FP8X4),
                lhsT_scale=scales[:, cols],
                rhs=x_code[:].bitcast(FP8X4),
                rhs_scale=x_scale[:],
                start=True,
                stop=True,
            )
            return acc

        weight = []
        squash = keep.tile([P, PACK, 2, USERS], F32, name="squash", tag="raw0", align_bytes=64)
        gap = keep.tile([P, PACK, USERS], F32, name="gap", tag="w1_dealt", align_bytes=64)
        for t in range(PACK):
            yd = layer(t, w2_codes, w2_scales, t)
            nc.scalar.activation(out=squash[:, t], in_=yd[:].rearrange("p v d -> p d v"), func=ACT.Sigmoid, scale=2.0)
            nc.vector.tensor_tensor(out=gap[:, t, :], in0=squash[:, t, 0, :], in1=squash[:, t, 1, :], op=ALU.subtract)
            share = keep.tile([P, USERS], F32, name="share%d" % t)
            nc.scalar.activation(out=share[:], in_=gap[:, t, :], func=ACT.Sigmoid, scale=2.2)
            weight.append(share)

        neg_user = keep.tile([P, PACK, USERS], F32, name="neg_user")
        similar = [keep.tile([P, PACK, P], F32, name="similar%d" % h) for h in range(BLOCKS)]
        for t in range(PACK):
            y = layer(4 + t, w1_codes, w1_scales, t)
            first = keep.tile([P, USERS], F32, name="first%d" % t)
            second = keep.tile([P, USERS], F32, name="second%d" % t, tag="second%d" % t, align_bytes=64)
            factor = unit_sb[:, t : t + 1]
            nc.vector.scalar_tensor_tensor(
                out=first[:], in0=y[:, :, 0], scalar=factor, in1=weight[t][:], op0=ALU.mult, op1=ALU.mult
            )
            nc.vector.scalar_tensor_tensor(
                out=second[:], in0=weight[t][:], scalar=1.0, in1=y[:, :, 1], op0=ALU.subtract, op1=ALU.mult
            )
            nc.vector.scalar_tensor_tensor(
                out=neg_user[:, t, :], in0=second[:], scalar=factor, in1=first[:], op0=ALU.mult, op1=ALU.subtract
            )
            for h in range(BLOCKS):
                nc.scalar.activation(
                    out=similar[h][:, t, :],
                    in_=neg_user[:, t, :].indirect(sim_sb[:, 8 * h : 8 * (h + 1)]),
                    func=ACT.Copy,
                    scale=0.6,
                )

        e_code = []
        for u in range(2):
            picked = keep.tile([P, ITEMS // 2], U32, name="e_code%d" % u, tag=["e_code0", "second3"][u], align_bytes=64)
            nc.vector.tensor_copy(out=picked[:], in_=e_word_table[:].indirect(itm_sb[:, 16 * u : 16 * (u + 1)]))
            e_code.append(picked)

        for h in range(BLOCKS):
            users = slice(h * P, (h + 1) * P)
            hid = keep.tile([P, P, PACK], BF16, name="hid%d" % h, align_bytes=64)
            nc.vector.tensor_tensor(
                out=hid[:].rearrange("p (c i) t -> p c t i", i=4),
                in0=similar[h][:].rearrange("p t (c i) -> p c t i", i=4),
                in1=neg_user[:, :, users].rearrange("p t (c i) -> p c t i", i=4),
                op=ALU.subtract,
            )
            hid_codes = keep.tile([P, P], U32, name="hid_codes%d" % h, align_bytes=64)
            hid_scales = keep.tile([P, P], U8, name="hid_scales%d" % h, align_bytes=64)
            nc.vector.quantize_mx(
                out=hid_codes[:].bitcast(FP8X4), scales=hid_scales[:], in_=hid[:].rearrange("p v t -> p (v t)")
            )
            score = bank(h, [P, ITEMS])
            for u in range(2):
                items = slice(u * ITEMS // 2, (u + 1) * ITEMS // 2)
                nc.tensor.matmul_mx(
                    out=score[:, items],
                    lhsT=hid_codes[:].bitcast(FP8X4),
                    lhsT_scale=hid_scales[:],
                    rhs=e_code[u][:].bitcast(FP8X4),
                    rhs_scale=e_scale[E_ROW0:, items],
                    start=True,
                    stop=True,
                )
            scaled = keep.tile([P, ITEMS], BF16, name="scaled%d" % h)
            mean = keep.tile([P, 1], F32, name="mean%d" % h)
            nc.scalar.activation(out=scaled[:], in_=score[:], func=ACT.Copy, scale=1.0 / ITEMS, accum_out=mean[:])
            for u in range(1 + h):
                width = ITEMS // (1 + h)
                items = slice(u * width, (u + 1) * width)
                result = keep.tile([P, width], F32, name="result%d_%d" % (h, u))
                nc.vector.scalar_tensor_tensor(
                    out=result[:], in0=score[:, items], scalar=mean[:], in1=inv_pop[:, items], op0=ALU.subtract, op1=ALU.mult
                )
                [nc.sync, nc.scalar][(h + u) % 2].dma_start(out=out[users, items], in_=result[:])
